import numpy as np
import ml_dtypes


def mxq(x, axis, fmt="e4m3"):
    dtype, down = {"e4m3": (ml_dtypes.float8_e4m3fn, 7), "e5m2": (ml_dtypes.float8_e5m2, 14)}[fmt]
    v = np.moveaxis(np.asarray(x, np.float32).astype(ml_dtypes.bfloat16).astype(np.float64), axis, -1)
    blocks = v.reshape(v.shape[:-1] + (-1, 32))
    amax = np.abs(blocks).max(-1, keepdims=True)
    byte = np.maximum(np.where(amax > 0, np.frexp(amax)[1] - 1 + 127, 0) - down, 1)
    scale = np.exp2(byte - 127.0)
    codes = (blocks / scale).astype(np.float32).astype(dtype).astype(np.float64)
    return np.moveaxis((codes * scale).reshape(v.shape), -1, axis)


WIDE = False


def mx_kscale(k):
    if not WIDE:
        return np.ones(k)
    levels = np.array([30, -30])
    if k % 512:
        return np.exp2(np.random.permutation(np.resize(levels, k // 32))).repeat(32)
    a = np.empty((k // 512, 16))
    for p in range(k // 512):
        a[p, :8] = np.random.permutation(np.resize(levels, 8))
        for g in range(8):
            far = levels[np.abs(levels - a[p, g]) >= 10]
            a[p, g + 8] = far[np.random.randint(len(far))]
    return np.exp2(a.ravel()).repeat(32)


def f64(x):
    return np.asarray(x).astype(np.float64)


def striped(idx):
    return np.tile(np.asarray(idx).reshape(-1, 16).T, (8, 1)).astype(np.uint16)


def unstriped(offs):
    return offs[:16].T.reshape(-1).astype(np.int64)


E2M1 = np.array([0.0, 0.5, 1.0, 1.5, 2.0, 3.0, 4.0, 6.0, -0.0, -0.5, -1.0, -1.5, -2.0, -3.0, -4.0, -6.0])


def pack_weight(w, fmt):
    k, n = w.shape
    w = f64(np.asarray(w, np.float32).astype(ml_dtypes.bfloat16)).reshape(k // 32, 32, n)
    amax = np.abs(w).max(1)
    if fmt in ("e4m3", "e5m2"):
        byte = np.frexp(amax)[1] - 1 + 127 - (7 if fmt == "e4m3" else 14)
    else:
        mant, ex = np.frexp(amax / 6.0)
        byte = np.where(mant > 0.5, ex, ex - 1) + 127
    byte = np.clip(np.where(amax > 0, byte, 1), 1, 254)
    scaled = (w * np.exp2(127.0 - byte)[:, None, :]).reshape(k, n).astype(np.float32)
    by_word = np.ascontiguousarray(scaled.reshape(k // 512, 128, 4, n).transpose(0, 1, 3, 2))
    if fmt in ("e4m3", "e5m2"):
        words = by_word.astype(ml_dtypes.float8_e4m3fn if fmt == "e4m3" else ml_dtypes.float8_e5m2).view(np.uint8)
    else:
        c = by_word.astype(ml_dtypes.float4_e2m1fn).view(np.uint8) & 0xF
        words = (c[..., 0::2] | (c[..., 1::2] << 4)).reshape(k // 512, 128, 2 * n)
    return np.ascontiguousarray(words), np.ascontiguousarray(byte.astype(np.uint8).reshape(k // 512, 16, n))


def unpack_weight(words, scales, fmt):
    g, _, n = scales.shape
    words = np.ascontiguousarray(words).reshape(g, 128, n, -1)
    if fmt in ("e4m3", "e5m2"):
        vals = words.view(ml_dtypes.float8_e4m3fn if fmt == "e4m3" else ml_dtypes.float8_e5m2).astype(np.float64)
    else:
        nib = np.empty((g, 128, n, 4), np.uint8)
        nib[..., 0::2] = words & 0xF
        nib[..., 1::2] = words >> 4
        vals = E2M1[nib]
    vals = vals * np.repeat(np.exp2(scales.astype(np.float64) - 127.0), 8, axis=1)[..., None]
    return vals.transpose(0, 1, 3, 2).reshape(g * 512, n)


def bf(x):
    return np.asarray(x, np.float32).astype(ml_dtypes.bfloat16)


def planes(Y):
    r, m = Y.shape
    b = f64(bf(Y)).reshape(r // 32, 32, m)
    amax = np.abs(b).max(1)
    byte = np.clip(np.where(amax > 0, np.frexp(amax)[1] - 1 + 127 - 7, 1), 1, 254)
    codes = (b * np.exp2(127.0 - byte)[:, None, :]).reshape(r, m).astype(np.float32).astype(ml_dtypes.float8_e4m3fn).view(np.uint8)
    words = codes.reshape(r // 512, 128, 4, m).transpose(0, 1, 3, 2)
    return np.ascontiguousarray(words), np.ascontiguousarray(byte.astype(np.uint8).reshape(r // 512, 16, m))


K, T, J, R, N = 1024, 1024, 256, 512, 512


def setup_inputs():
    n = np.random.standard_normal
    idx = np.random.permutation(T)[:J]
    idx2 = np.random.permutation(T)[:J]
    fk = mx_kscale(K)
    fr = mx_kscale(R)
    wp = pack_weight(n((K, R)) * 1 / np.sqrt(K) * fk[:, None] * fr, "e2m1")
    wbp = pack_weight(n((R, N)) * np.random.uniform(0.3, 1.7, (1, N)) / np.sqrt(R) / fr[:, None], "e5m2")
    return {
        "xf": (n((K, T))).astype(np.float32),
        "fk": (np.random.uniform(0.5, 2.0, (K, 1)) / fk[:, None]).astype(np.float32),
        "w_words": wp[0],
        "w_scales": wp[1],
        "wb_words": wbp[0],
        "wb_scales": wbp[1],
        "rs": (0.6 * n((N, J)) + np.random.uniform(-1.0, 1.0, (N, 1))).astype(np.float32),
        "offs": striped(idx),
        "offs2": striped(idx2),
    }


def reference(xf, fk, w_words, w_scales, wb_words, wb_scales, rs, offs, offs2):
    idx = unstriped(offs)
    idx2 = unstriped(offs2)
    wu = unpack_weight(w_words, w_scales, "e2m1")
    wbu = unpack_weight(wb_words, wb_scales, "e5m2")
    u = (f64(xf)[:, idx] - f64(xf)[:, idx2]) * f64(fk)
    uq = mxq(u, 0, "e4m3")
    a = wu.T @ uq
    ha = np.maximum(a, 0.0)
    h1 = np.pad(ha, ((0, 0), (2, 0)))[:, :J]
    hid = ha - 0.5 * h1
    hidq = mxq(hid, 0, "e5m2")
    p = wbu.T @ hidq
    pb = p + f64(rs)
    mn = np.mean(pb, axis=1, keepdims=True)
    d = pb - mn
    y = d / np.sqrt(np.mean(np.square(d), axis=1, keepdims=True) + 0.1)
    words, scales = planes(y)
    return y, words, scales

@@ -1,0 +1,256 @@
+from contextlib import ExitStack
+
+import concourse.mybir as mybir
+
+K, T, J, R, N = 1024, 1024, 256, 512, 512
+FLOPS = 2 * K * R * J + 2 * R * N * J
+
+F32 = mybir.dt.float32
+BF16 = mybir.dt.bfloat16
+I32 = mybir.dt.int32
+U32 = mybir.dt.uint32
+U16 = mybir.dt.uint16
+U8 = mybir.dt.uint8
+E4M3 = mybir.dt.float8_e4m3fn_x4
+E5M2 = mybir.dt.float8_e5m2_x4
+E2M1 = mybir.dt.float4_e2m1fn_x4
+ALU = mybir.AluOpType
+ACT = mybir.ActivationFunctionType
+
+P = 128
+PACK = 4
+PASSES = K // (P * PACK)
+HALF = J // 2
+LAG = 2
+BOTH_ON_SCALAR = [0,1]
+
+
+def tile_list_pickgaps_lagged_levelled_pl_kernel(
+    tc, xf, fk, w_words, w_scales, wb_words, wb_scales, rs, offs, offs2, out_0, out_1, out_2
+):
+    nc = tc.nc
+    with ExitStack() as ctx:
+        keep = ctx.enter_context(tc.tile_pool(name="keep", bufs=1))
+        psum = ctx.enter_context(tc.psum_pool(name="psum", bufs=1))
+
+        first = keep.tile([P, J // 16], U16, name="first")
+        second = keep.tile([P, J // 16], U16, name="second")
+        factor = keep.tile([P, PASSES, PACK], F32, name="factor")
+        rows = [[keep.tile([P, T], F32, name=f"rows{a}{t}") for t in range(PACK)] for a in range(PASSES)]
+        w_raw = [keep.tile([P, 2 * R], U8, name=f"w_raw{a}") for a in range(PASSES)]
+        ws_raw = keep.tile([P, PASSES, R], U8, name="ws_raw")
+        wb_raw = keep.tile([P, N], U32, name="wb_raw")
+        wbs_raw = keep.tile([P, N], U8, name="wbs_raw")
+        resid = keep.tile([P, PACK, J], F32, name="resid")
+        ha = keep.tile([P, (LAG + J) * PACK], F32, name="ha")
+
+        nc.gpsimd.memset(ws_raw[:].bitcast(U32), 0)
+        nc.gpsimd.memset(wbs_raw[:].bitcast(U32), 0)
+        nc.gpsimd.memset(ha[:, 0 : LAG * PACK], 0.0)
+
+        x_rows = xf.rearrange("(a p t) c -> a t p c", p=P, t=PACK)
+
+        def load_rows(i):
+            nc.sync.dma_start(out=rows[i // PACK][i % PACK][:], in_=x_rows[i // PACK, i % PACK])
+
+        def load_w_scales(q):
+            nc.sync.dma_start(
+                out=ws_raw[32 * q : 32 * q + 4, :, :].bitcast(I32),
+                in_=w_scales[:, 4 * q : 4 * q + 4, :].rearrange("a r c -> r a c").bitcast(I32),
+            )
+
+        def load_w(a):
+            nc.sync.dma_start(out=w_raw[a][:].bitcast(I32), in_=w_words[a].bitcast(I32))
+
+        load_rows(0)
+        nc.sync.dma_start(second[:], offs2)
+        nc.sync.dma_start(first[:], offs)
+        load_rows(1)
+        nc.sync.dma_start(out=factor[:], in_=fk.rearrange("(a p t) o -> p a (t o)", p=P, t=PACK))
+        load_rows(2)
+        for q in range(4):
+            load_w_scales(q)
+        load_rows(3)
+        load_w(0)
+        load_rows(4)
+        load_w(1)
+        for i in range(5, PASSES * PACK):
+            load_rows(i)
+        nc.sync.dma_start(out=wb_raw[:].bitcast(I32), in_=wb_words[0].rearrange("p c t -> p (c t)").bitcast(I32))
+        for q in range(4):
+            nc.sync.dma_start(
+                out=wbs_raw[32 * q : 32 * q + 4, :].bitcast(I32),
+                in_=wb_scales[0, 4 * q : 4 * q + 4, :].bitcast(I32),
+            )
+        nc.sync.dma_start(out=resid[:], in_=rs.rearrange("(p t) j -> p t j", t=PACK))
+
+        w_codes = [keep.tile([P, 2 * R], U8, name=f"w_codes{a}", align_bytes=64) for a in range(PASSES)]
+        w_plane = keep.tile([P, PASSES, R], U8, name="w_plane", align_bytes=64)
+        wb_codes = keep.tile([P, N], U32, name="wb_codes", align_bytes=64)
+        wb_plane = keep.tile([P, N], U8, name="wb_plane", align_bytes=64)
+
+        def deal(copy, dst, src, run):
+            copy(
+                out=dst.rearrange("p (t c i) -> p c t i", t=PACK, i=run),
+                in_=src.rearrange("p (c i t) -> p c t i", t=PACK, i=run),
+            )
+
+        halves = [slice(h * HALF, (h + 1) * HALF) for h in range(2)]
+        list_halves = [slice(h * HALF // 16, (h + 1) * HALF // 16) for h in range(2)]
+        a_banks = [psum.tile([P, PACK, HALF], F32, name=f"a_bank{h}") for h in range(2)]
+        p_banks = [psum.tile([P, J], F32, name=f"p_bank{t}") for t in range(PACK)]
+
+        u_codes = [keep.tile([P, J], U32, name=f"u_codes{a}", align_bytes=64) for a in range(PASSES)]
+        u_plane = [keep.tile([P, J], U8, name=f"u_plane{a}", align_bytes=64) for a in range(PASSES)]
+        for a in range(PASSES):
+            scaled = keep.tile([P, PACK - 1, J], BF16, name=f"scaled{a}")
+            u = keep.tile([P, J, PACK], BF16, name=f"u{a}", align_bytes=64)
+            for t in range(PACK):
+                taken = keep.tile([P, J], F32, name=f"taken{a}{t}")
+                gap = keep.tile([P, J], F32, name=f"gap{a}{t}")
+                window = rows[a][t][:]
+                f = factor[:, a, t : t + 1]
+                if t < PACK - 1:
+                    nc.scalar.activation(out=taken[:], in_=window.indirect(second[:]), func=ACT.Copy)
+                    if t in BOTH_ON_SCALAR:
+                        picked = keep.tile([P, J], F32, name=f"picked{a}{t}")
+                        nc.scalar.activation(out=picked[:], in_=window.indirect(first[:]), func=ACT.Copy)
+                        nc.vector.tensor_tensor(out=gap[:], in0=picked[:], in1=taken[:], op=ALU.subtract)
+                    else:
+                        nc.vector.tensor_tensor(out=gap[:], in0=window.indirect(first[:]), in1=taken[:], op=ALU.subtract)
+                    nc.vector.tensor_scalar(out=scaled[:, t, :], in0=gap[:], scalar1=f, scalar2=None, op0=ALU.mult)
+                else:
+                    nc.vector.tensor_copy(
+                        out=u[:, :, 0 : PACK - 1].rearrange("p (c i) t -> p c t i", i=4),
+                        in_=scaled[:].rearrange("p t (c i) -> p c t i", i=4),
+                    )
+                    for h in range(2):
+                        nc.scalar.activation(
+                            out=taken[:, halves[h]], in_=window.indirect(second[:, list_halves[h]]), func=ACT.Copy
+                        )
+                    for h in range(2):
+                        nc.vector.tensor_tensor(
+                            out=gap[:, halves[h]],
+                            in0=window.indirect(first[:, list_halves[h]]),
+                            in1=taken[:, halves[h]],
+                            op=ALU.subtract,
+                        )
+                    for h in range(2):
+                        nc.vector.tensor_scalar(
+                            out=u[:, halves[h], t], in0=gap[:, halves[h]], scalar1=f, scalar2=None, op0=ALU.mult
+                        )
+            for h in range(2):
+                nc.vector.quantize_mx(
+                    out=u_codes[a][:, halves[h]].bitcast(E4M3),
+                    scales=u_plane[a][:, halves[h]],
+                    in_=u[:, halves[h], :].rearrange("p j t -> p (j t)"),
+                )
+            if a == 0:
+                for b in range(PASSES):
+                    deal(nc.vector.tensor_copy, w_plane[:, b, :], ws_raw[:, b, :], 16)
+                deal(nc.scalar.copy, w_codes[0][:].bitcast(U16), w_raw[0][:].bitcast(U16), 8)
+                deal(nc.scalar.copy, w_codes[1][:].bitcast(U16), w_raw[1][:].bitcast(U16), 8)
+
+
+        for h, a in [(h, a) for a in range(PASSES) for h in range(2)]:
+            for t in range(PACK):
+                nc.tensor.matmul_mx(
+                    out=a_banks[h][:, t, :],
+                    lhsT=w_codes[a][:, 2 * P * t : 2 * P * (t + 1)].bitcast(E2M1),
+                    lhsT_scale=w_plane[:, a, P * t : P * (t + 1)],
+                    rhs=u_codes[a][:, halves[h]].bitcast(E4M3),
+                    rhs_scale=u_plane[a][:, halves[h]],
+                    start=(a == 0 and t == 0),
+                    stop=(a == PASSES - 1 and t == PACK - 1),
+                )
+
+        deal(nc.scalar.copy, wb_codes[:], wb_raw[:], 4)
+        deal(nc.vector.tensor_copy, wb_plane[:], wbs_raw[:], 16)
+
+        hid = keep.tile([P, J * PACK], BF16, name="hid", align_bytes=64)
+        hid_codes = keep.tile([P, J], U32, name="hid_codes", align_bytes=64)
+        hid_plane = keep.tile([P, J], U8, name="hid_plane", align_bytes=64)
+        pieces = 1
+        width = HALF // pieces
+        span = width * PACK
+        for h in range(2):
+            for c in range(pieces):
+                at = (h * pieces + c) * span
+                now = ha[:, LAG * PACK + at : LAG * PACK + at + span]
+                before = ha[:, at : at + span]
+                nc.scalar.activation(
+                    out=now.rearrange("p (j t) -> p j t", t=PACK),
+                    in_=a_banks[h][:, :, c * width : (c + 1) * width].rearrange("p t j -> p j t"),
+                    func=ACT.Relu,
+                )
+                nc.vector.scalar_tensor_tensor(
+                    out=hid[:, at : at + span], in0=before, scalar=-0.5, in1=now, op0=ALU.mult, op1=ALU.add
+                )
+        for h in range(2):
+            nc.vector.quantize_mx(
+                out=hid_codes[:, halves[h]].bitcast(E5M2),
+                scales=hid_plane[:, halves[h]],
+                in_=hid[:, h * HALF * PACK : (h + 1) * HALF * PACK],
+            )
+            for t in range(PACK):
+                nc.tensor.matmul_mx(
+                    out=p_banks[t][:, halves[h]],
+                    lhsT=wb_codes[:, P * t : P * (t + 1)].bitcast(E5M2),
+                    lhsT_scale=wb_plane[:, P * t : P * (t + 1)],
+                    rhs=hid_codes[:, halves[h]].bitcast(E5M2),
+                    rhs_scale=hid_plane[:, halves[h]],
+                    start=True,
+                    stop=True,
+                )
+
+        pb = keep.tile([P, PACK, J], F32, name="pb")
+        squares = keep.tile([P, PACK, J], BF16, name="squares")
+        total = keep.tile([P, PACK], F32, name="total")
+        energy = keep.tile([P, PACK], F32, name="energy")
+        mean = keep.tile([P, PACK], F32, name="mean")
+        spread = keep.tile([P, PACK], F32, name="spread")
+        inverse = keep.tile([P, PACK], F32, name="inverse")
+        y = keep.tile([P, PACK, J], F32, name="y")
+        y_rows = out_0.rearrange("(p t) j -> p t j", t=PACK)
+        pairs = [slice(0, 2), slice(2, 4)]
+        for pair in pairs:
+            for t in range(pair.start, pair.stop):
+                nc.vector.scalar_tensor_tensor(
+                    out=pb[:, t, :], in0=p_banks[t][:], scalar=1.0, in1=resid[:, t, :],
+                    op0=ALU.mult, op1=ALU.add, accum_out=total[:, t : t + 1],
+                )
+                nc.scalar.activation(
+                    out=squares[:, t, :], in_=pb[:, t, :], func=ACT.Square,
+                    scale=-float(J), bias=total[:, t : t + 1], accum_out=energy[:, t : t + 1],
+                )
+            nc.scalar.activation(out=spread[:, pair], in_=energy[:, pair], func=ACT.Sqrt, scale=1.0 / J**3, bias=0.1)
+        nc.vector.tensor_scalar(out=mean[:], in0=total[:], scalar1=1.0 / J, scalar2=None, op0=ALU.mult)
+        for pair in pairs:
+            nc.vector.reciprocal(out=inverse[:, pair], in_=spread[:, pair])
+            for t in range(pair.start, pair.stop):
+                nc.vector.tensor_scalar(
+                    out=y[:, t, :], in0=pb[:, t, :], scalar1=mean[:, t : t + 1], scalar2=inverse[:, t : t + 1],
+                    op0=ALU.subtract, op1=ALU.mult,
+                )
+            nc.sync.dma_start(out=y_rows[:, pair, :], in_=y[:, pair, :])
+
+        y_round = keep.tile([P, J, PACK], BF16, name="y_round", align_bytes=64)
+        y_codes = keep.tile([P, J], U32, name="y_codes", align_bytes=64)
+        y_plane = keep.tile([P, J], U8, name="y_plane", align_bytes=64)
+        for h, copy in enumerate((nc.vector.tensor_copy, nc.scalar.copy)):
+            copy(
+                out=y_round[:, halves[h], :].rearrange("p (c i) t -> p c t i", i=4),
+                in_=y[:, :, halves[h]].rearrange("p t (c i) -> p c t i", i=4),
+            )
+        for h in range(2):
+            nc.vector.quantize_mx(
+                out=y_codes[:, halves[h]].bitcast(E4M3),
+                scales=y_plane[:, halves[h]],
+                in_=y_round[:, halves[h], :].rearrange("p j t -> p (j t)"),
+            )
+        nc.sync.dma_start(out=out_1[0].rearrange("p c t -> p (c t)").bitcast(I32), in_=y_codes[:].bitcast(I32))
+        for q in range(4):
+            queue = nc.scalar if q % 2 == 0 else nc.sync
+            queue.dma_start(
+                out=out_2[0, 4 * q : 4 * q + 4, :].bitcast(I32), in_=y_plane[32 * q : 32 * q + 4, :].bitcast(I32)
+            )

@@ -20,9 +20,33 @@ ACT = mybir.ActivationFunctionType
 P = 128
 PACK = 4
 PASSES = K // (P * PACK)
+SHEETS = PASSES * PACK
+QUADRANT = 32
+ENTRIES = 16
+LINE = 16
 HALF = J // 2
+QUARTER = J // 4
 LAG = 2
-BOTH_ON_SCALAR = [0,1]
+EPS = 0.1
+
+BOTH_ON_SCALAR = (1, 3, 4, 5)
+BY_HALVES = (0, SHEETS - 3, SHEETS - 2, SHEETS - 1)
+WOVEN_BY_VECTOR = 160
+
+
+def deal(copy, dealt, raw, width):
+    run = LINE // width
+    copy(
+        out=dealt.rearrange("p (t c i) -> p c t i", t=PACK, i=run),
+        in_=raw.rearrange("p (c i t) -> p c t i", t=PACK, i=run),
+    )
+
+
+def load_scale_rows(queue, tile, rows, q):
+    queue.dma_start(
+        out=tile[QUADRANT * q : QUADRANT * q + 4, :, :].bitcast(I32),
+        in_=rows[:, 4 * q : 4 * q + 4, :].rearrange("a s c -> s a c").bitcast(I32),
+    )
 
 
 def tile_list_pickgaps_lagged_levelled_pl_kernel(
@@ -33,172 +57,141 @@ def tile_list_pickgaps_lagged_levelled_pl_kernel(
         keep = ctx.enter_context(tc.tile_pool(name="keep", bufs=1))
         psum = ctx.enter_context(tc.psum_pool(name="psum", bufs=1))
 
-        first = keep.tile([P, J // 16], U16, name="first")
-        second = keep.tile([P, J // 16], U16, name="second")
+        first = keep.tile([P, J // ENTRIES], U16, name="first")
+        second = keep.tile([P, J // ENTRIES], U16, name="second")
         factor = keep.tile([P, PASSES, PACK], F32, name="factor")
-        rows = [[keep.tile([P, T], F32, name=f"rows{a}{t}") for t in range(PACK)] for a in range(PASSES)]
+        sheets = [keep.tile([P, T], F32, name=f"sheet{s}") for s in range(SHEETS)]
         w_raw = [keep.tile([P, 2 * R], U8, name=f"w_raw{a}") for a in range(PASSES)]
-        ws_raw = keep.tile([P, PASSES, R], U8, name="ws_raw")
-        wb_raw = keep.tile([P, N], U32, name="wb_raw")
-        wbs_raw = keep.tile([P, N], U8, name="wbs_raw")
+        w_scales_raw = keep.tile([P, PASSES, R], U8, name="w_scales_raw")
+        wb_raw = keep.tile([P, N], U32, name="wb_raw", tag="wb_raw", align_bytes=64)
+        wb_scales_raw = keep.tile([P, 1, N], U8, name="wb_scales_raw")
         resid = keep.tile([P, PACK, J], F32, name="resid")
         ha = keep.tile([P, (LAG + J) * PACK], F32, name="ha")
 
-        nc.gpsimd.memset(ws_raw[:].bitcast(U32), 0)
-        nc.gpsimd.memset(wbs_raw[:].bitcast(U32), 0)
+        nc.gpsimd.memset(w_scales_raw[:].bitcast(U32), 0)
+        nc.gpsimd.memset(wb_scales_raw[:].bitcast(U32), 0)
         nc.gpsimd.memset(ha[:, 0 : LAG * PACK], 0.0)
 
         x_rows = xf.rearrange("(a p t) c -> a t p c", p=P, t=PACK)
 
-        def load_rows(i):
-            nc.sync.dma_start(out=rows[i // PACK][i % PACK][:], in_=x_rows[i // PACK, i % PACK])
+        def load_sheet(s):
+            nc.sync.dma_start(out=sheets[s][:], in_=x_rows[s // PACK, s % PACK])
 
-        def load_w_scales(q):
-            nc.sync.dma_start(
-                out=ws_raw[32 * q : 32 * q + 4, :, :].bitcast(I32),
-                in_=w_scales[:, 4 * q : 4 * q + 4, :].rearrange("a r c -> r a c").bitcast(I32),
-            )
-
-        def load_w(a):
-            nc.sync.dma_start(out=w_raw[a][:].bitcast(I32), in_=w_words[a].bitcast(I32))
-
-        load_rows(0)
+        load_sheet(0)
         nc.sync.dma_start(second[:], offs2)
         nc.sync.dma_start(first[:], offs)
-        load_rows(1)
+        for q in range(P // QUADRANT):
+            load_scale_rows(nc.scalar, w_scales_raw, w_scales, q)
+        load_sheet(1)
+        load_sheet(2)
         nc.sync.dma_start(out=factor[:], in_=fk.rearrange("(a p t) o -> p a (t o)", p=P, t=PACK))
-        load_rows(2)
-        for q in range(4):
-            load_w_scales(q)
-        load_rows(3)
-        load_w(0)
-        load_rows(4)
-        load_w(1)
-        for i in range(5, PASSES * PACK):
-            load_rows(i)
+        for s in range(3, SHEETS):
+            load_sheet(s)
+        for a in range(PASSES):
+            nc.sync.dma_start(out=w_raw[a][:].bitcast(I32), in_=w_words[a].bitcast(I32))
         nc.sync.dma_start(out=wb_raw[:].bitcast(I32), in_=wb_words[0].rearrange("p c t -> p (c t)").bitcast(I32))
-        for q in range(4):
-            nc.sync.dma_start(
-                out=wbs_raw[32 * q : 32 * q + 4, :].bitcast(I32),
-                in_=wb_scales[0, 4 * q : 4 * q + 4, :].bitcast(I32),
-            )
+        for q in range(P // QUADRANT):
+            load_scale_rows(nc.sync, wb_scales_raw, wb_scales, q)
         nc.sync.dma_start(out=resid[:], in_=rs.rearrange("(p t) j -> p t j", t=PACK))
+
+        one = keep.tile([P, 1], F32, name="one")
+        unread = keep.tile([P, 1], F32, name="unread")
+        nc.vector.memset(one[:], 1.0)
+        nc.scalar.activation(out=unread[:], in_=one[:], func=ACT.Abs_reciprocal_sqrt)
 
         w_codes = [keep.tile([P, 2 * R], U8, name=f"w_codes{a}", align_bytes=64) for a in range(PASSES)]
         w_plane = keep.tile([P, PASSES, R], U8, name="w_plane", align_bytes=64)
-        wb_codes = keep.tile([P, N], U32, name="wb_codes", align_bytes=64)
-        wb_plane = keep.tile([P, N], U8, name="wb_plane", align_bytes=64)
+        nc.vector.tensor_copy(
+            out=w_plane[:].rearrange("p a (t c i) -> p a c t i", t=PACK, i=LINE),
+            in_=w_scales_raw[:].rearrange("p a (c i t) -> p a c t i", t=PACK, i=LINE),
+        )
 
-        def deal(copy, dst, src, run):
-            copy(
-                out=dst.rearrange("p (t c i) -> p c t i", t=PACK, i=run),
-                in_=src.rearrange("p (c i t) -> p c t i", t=PACK, i=run),
-            )
-
+        whole = slice(0, J)
         halves = [slice(h * HALF, (h + 1) * HALF) for h in range(2)]
-        list_halves = [slice(h * HALF // 16, (h + 1) * HALF // 16) for h in range(2)]
-        a_banks = [psum.tile([P, PACK, HALF], F32, name=f"a_bank{h}") for h in range(2)]
-        p_banks = [psum.tile([P, J], F32, name=f"p_bank{t}") for t in range(PACK)]
+
+        def picks(window, offsets, slots):
+            return window[:].indirect(offsets[:, slots.start // ENTRIES : slots.stop // ENTRIES])
 
         u_codes = [keep.tile([P, J], U32, name=f"u_codes{a}", align_bytes=64) for a in range(PASSES)]
         u_plane = [keep.tile([P, J], U8, name=f"u_plane{a}", align_bytes=64) for a in range(PASSES)]
         for a in range(PASSES):
-            scaled = keep.tile([P, PACK - 1, J], BF16, name=f"scaled{a}")
-            u = keep.tile([P, J, PACK], BF16, name=f"u{a}", align_bytes=64)
+            u = keep.tile([P, J, PACK], BF16, name=f"u{a}", tag=f"u{a}", align_bytes=64)
+            gaps = keep.tile([P, PACK, J], F32, name=f"gaps{a}")
             for t in range(PACK):
-                taken = keep.tile([P, J], F32, name=f"taken{a}{t}")
-                gap = keep.tile([P, J], F32, name=f"gap{a}{t}")
-                window = rows[a][t][:]
-                f = factor[:, a, t : t + 1]
-                if t < PACK - 1:
-                    nc.scalar.activation(out=taken[:], in_=window.indirect(second[:]), func=ACT.Copy)
-                    if t in BOTH_ON_SCALAR:
-                        picked = keep.tile([P, J], F32, name=f"picked{a}{t}")
-                        nc.scalar.activation(out=picked[:], in_=window.indirect(first[:]), func=ACT.Copy)
-                        nc.vector.tensor_tensor(out=gap[:], in0=picked[:], in1=taken[:], op=ALU.subtract)
-                    else:
-                        nc.vector.tensor_tensor(out=gap[:], in0=window.indirect(first[:]), in1=taken[:], op=ALU.subtract)
-                    nc.vector.tensor_scalar(out=scaled[:, t, :], in0=gap[:], scalar1=f, scalar2=None, op0=ALU.mult)
-                else:
-                    nc.vector.tensor_copy(
-                        out=u[:, :, 0 : PACK - 1].rearrange("p (c i) t -> p c t i", i=4),
-                        in_=scaled[:].rearrange("p t (c i) -> p c t i", i=4),
+                s = a * PACK + t
+                taken = keep.tile([P, J], F32, name=f"taken{s}")
+                if s in BOTH_ON_SCALAR:
+                    picked = keep.tile([P, J], F32, name=f"picked{s}")
+                for slots in halves if s in BY_HALVES else [whole]:
+                    nc.scalar.activation(out=taken[:, slots], in_=picks(sheets[s], second, slots), func=ACT.Copy)
+                    if s in BOTH_ON_SCALAR:
+                        nc.scalar.activation(out=picked[:, slots], in_=picks(sheets[s], first, slots), func=ACT.Copy)
+                for slots in halves:
+                    minuend = picked[:, slots] if s in BOTH_ON_SCALAR else picks(sheets[s], first, slots)
+                    nc.vector.tensor_tensor(out=gaps[:, t, slots], in0=minuend, in1=taken[:, slots], op=ALU.subtract)
+                for slots in halves:
+                    nc.vector.tensor_scalar(
+                        out=u[:, slots, t], in0=gaps[:, t, slots], scalar1=factor[:, a, t : t + 1],
+                        scalar2=None, op0=ALU.mult,
                     )
-                    for h in range(2):
-                        nc.scalar.activation(
-                            out=taken[:, halves[h]], in_=window.indirect(second[:, list_halves[h]]), func=ACT.Copy
-                        )
-                    for h in range(2):
-                        nc.vector.tensor_tensor(
-                            out=gap[:, halves[h]],
-                            in0=window.indirect(first[:, list_halves[h]]),
-                            in1=taken[:, halves[h]],
-                            op=ALU.subtract,
-                        )
-                    for h in range(2):
-                        nc.vector.tensor_scalar(
-                            out=u[:, halves[h], t], in0=gap[:, halves[h]], scalar1=f, scalar2=None, op0=ALU.mult
-                        )
-            for h in range(2):
+            for slots in halves if a == PASSES - 1 else [whole]:
                 nc.vector.quantize_mx(
-                    out=u_codes[a][:, halves[h]].bitcast(E4M3),
-                    scales=u_plane[a][:, halves[h]],
-                    in_=u[:, halves[h], :].rearrange("p j t -> p (j t)"),
-                )
-            if a == 0:
-                for b in range(PASSES):
-                    deal(nc.vector.tensor_copy, w_plane[:, b, :], ws_raw[:, b, :], 16)
-                deal(nc.scalar.copy, w_codes[0][:].bitcast(U16), w_raw[0][:].bitcast(U16), 8)
-                deal(nc.scalar.copy, w_codes[1][:].bitcast(U16), w_raw[1][:].bitcast(U16), 8)
-
-
-        for h, a in [(h, a) for a in range(PASSES) for h in range(2)]:
-            for t in range(PACK):
-                nc.tensor.matmul_mx(
-                    out=a_banks[h][:, t, :],
-                    lhsT=w_codes[a][:, 2 * P * t : 2 * P * (t + 1)].bitcast(E2M1),
-                    lhsT_scale=w_plane[:, a, P * t : P * (t + 1)],
-                    rhs=u_codes[a][:, halves[h]].bitcast(E4M3),
-                    rhs_scale=u_plane[a][:, halves[h]],
-                    start=(a == 0 and t == 0),
-                    stop=(a == PASSES - 1 and t == PACK - 1),
+                    out=u_codes[a][:, slots].bitcast(E4M3),
+                    scales=u_plane[a][:, slots],
+                    in_=u[:, slots, :].rearrange("p j t -> p (j t)"),
                 )
 
-        deal(nc.scalar.copy, wb_codes[:], wb_raw[:], 4)
-        deal(nc.vector.tensor_copy, wb_plane[:], wbs_raw[:], 16)
+        for a in range(PASSES):
+            deal(nc.scalar.copy, w_codes[a][:].bitcast(U16), w_raw[a][:].bitcast(U16), 2)
+        a_banks = [psum.tile([P, PACK, HALF], F32, name=f"a_bank{h}") for h in range(2)]
+        for a in range(PASSES):
+            for h, slots in enumerate(halves):
+                for t in range(PACK):
+                    nc.tensor.matmul_mx(
+                        out=a_banks[h][:, t, :],
+                        lhsT=w_codes[a][:, 2 * P * t : 2 * P * (t + 1)].bitcast(E2M1),
+                        lhsT_scale=w_plane[:, a, P * t : P * (t + 1)],
+                        rhs=u_codes[a][:, slots].bitcast(E4M3),
+                        rhs_scale=u_plane[a][:, slots],
+                        start=(a == 0 and t == 0),
+                        stop=(a == PASSES - 1 and t == PACK - 1),
+                    )
+
+        wb_codes = keep.tile([P, N], U32, name="wb_codes", tag=f"u{PASSES - 1}", align_bytes=64)
+        deal(nc.vector.tensor_copy, wb_codes[:].bitcast(I32), wb_raw[:].bitcast(I32), 4)
+        wb_plane = keep.tile([P, N], U8, name="wb_plane", tag="wb_raw", align_bytes=64)
+        deal(nc.vector.tensor_copy, wb_plane[:], wb_scales_raw[:, 0, :], 1)
 
         hid = keep.tile([P, J * PACK], BF16, name="hid", align_bytes=64)
         hid_codes = keep.tile([P, J], U32, name="hid_codes", align_bytes=64)
         hid_plane = keep.tile([P, J], U8, name="hid_plane", align_bytes=64)
-        pieces = 1
-        width = HALF // pieces
-        span = width * PACK
-        for h in range(2):
-            for c in range(pieces):
-                at = (h * pieces + c) * span
-                now = ha[:, LAG * PACK + at : LAG * PACK + at + span]
-                before = ha[:, at : at + span]
-                nc.scalar.activation(
-                    out=now.rearrange("p (j t) -> p j t", t=PACK),
-                    in_=a_banks[h][:, :, c * width : (c + 1) * width].rearrange("p t j -> p j t"),
-                    func=ACT.Relu,
-                )
-                nc.vector.scalar_tensor_tensor(
-                    out=hid[:, at : at + span], in0=before, scalar=-0.5, in1=now, op0=ALU.mult, op1=ALU.add
-                )
-        for h in range(2):
+        for j0 in range(0, J, QUARTER):
+            now = ha[:, (LAG + j0) * PACK : (LAG + j0 + QUARTER) * PACK]
+            before = ha[:, j0 * PACK : (j0 + QUARTER) * PACK]
+            nc.scalar.activation(
+                out=now.rearrange("p (j t) -> p j t", t=PACK),
+                in_=a_banks[j0 // HALF][:, :, j0 % HALF : j0 % HALF + QUARTER].rearrange("p t j -> p j t"),
+                func=ACT.Relu,
+            )
+            nc.vector.scalar_tensor_tensor(
+                out=hid[:, j0 * PACK : (j0 + QUARTER) * PACK], in0=before, scalar=-0.5, in1=now,
+                op0=ALU.mult, op1=ALU.add,
+            )
+
+        p_banks = [psum.tile([P, J], F32, name=f"p_bank{t}") for t in range(PACK)]
+        for slots in halves:
             nc.vector.quantize_mx(
-                out=hid_codes[:, halves[h]].bitcast(E5M2),
-                scales=hid_plane[:, halves[h]],
-                in_=hid[:, h * HALF * PACK : (h + 1) * HALF * PACK],
+                out=hid_codes[:, slots].bitcast(E5M2),
+                scales=hid_plane[:, slots],
+                in_=hid[:, slots.start * PACK : slots.stop * PACK],
             )
             for t in range(PACK):
                 nc.tensor.matmul_mx(
-                    out=p_banks[t][:, halves[h]],
+                    out=p_banks[t][:, slots],
                     lhsT=wb_codes[:, P * t : P * (t + 1)].bitcast(E5M2),
                     lhsT_scale=wb_plane[:, P * t : P * (t + 1)],
-                    rhs=hid_codes[:, halves[h]].bitcast(E5M2),
-                    rhs_scale=hid_plane[:, halves[h]],
+                    rhs=hid_codes[:, slots].bitcast(E5M2),
+                    rhs_scale=hid_plane[:, slots],
                     start=True,
                     stop=True,
                 )
@@ -208,13 +201,12 @@ def tile_list_pickgaps_lagged_levelled_pl_kernel(
         total = keep.tile([P, PACK], F32, name="total")
         energy = keep.tile([P, PACK], F32, name="energy")
         mean = keep.tile([P, PACK], F32, name="mean")
-        spread = keep.tile([P, PACK], F32, name="spread")
         inverse = keep.tile([P, PACK], F32, name="inverse")
         y = keep.tile([P, PACK, J], F32, name="y")
         y_rows = out_0.rearrange("(p t) j -> p t j", t=PACK)
-        pairs = [slice(0, 2), slice(2, 4)]
-        for pair in pairs:
-            for t in range(pair.start, pair.stop):
+        groups = [slice(0, 2), slice(2, 3), slice(3, 4)]
+        for group in groups:
+            for t in range(group.start, group.stop):
                 nc.vector.scalar_tensor_tensor(
                     out=pb[:, t, :], in0=p_banks[t][:], scalar=1.0, in1=resid[:, t, :],
                     op0=ALU.mult, op1=ALU.add, accum_out=total[:, t : t + 1],
@@ -223,34 +215,33 @@ def tile_list_pickgaps_lagged_levelled_pl_kernel(
                     out=squares[:, t, :], in_=pb[:, t, :], func=ACT.Square,
                     scale=-float(J), bias=total[:, t : t + 1], accum_out=energy[:, t : t + 1],
                 )
-            nc.scalar.activation(out=spread[:, pair], in_=energy[:, pair], func=ACT.Sqrt, scale=1.0 / J**3, bias=0.1)
+            nc.scalar.activation(
+                out=inverse[:, group], in_=energy[:, group], func=ACT.Abs_reciprocal_sqrt, scale=1.0 / J**3, bias=EPS
+            )
         nc.vector.tensor_scalar(out=mean[:], in0=total[:], scalar1=1.0 / J, scalar2=None, op0=ALU.mult)
-        for pair in pairs:
-            nc.vector.reciprocal(out=inverse[:, pair], in_=spread[:, pair])
-            for t in range(pair.start, pair.stop):
-                nc.vector.tensor_scalar(
-                    out=y[:, t, :], in0=pb[:, t, :], scalar1=mean[:, t : t + 1], scalar2=inverse[:, t : t + 1],
-                    op0=ALU.subtract, op1=ALU.mult,
-                )
-            nc.sync.dma_start(out=y_rows[:, pair, :], in_=y[:, pair, :])
+        for t in range(PACK):
+            nc.vector.tensor_scalar(
+                out=y[:, t, :], in0=pb[:, t, :], scalar1=mean[:, t : t + 1], scalar2=inverse[:, t : t + 1],
+                op0=ALU.subtract, op1=ALU.mult,
+            )
+            if t % 2 == 1:
+                nc.sync.dma_start(out=y_rows[:, t - 1 : t + 1, :], in_=y[:, t - 1 : t + 1, :])
 
         y_round = keep.tile([P, J, PACK], BF16, name="y_round", align_bytes=64)
         y_codes = keep.tile([P, J], U32, name="y_codes", align_bytes=64)
         y_plane = keep.tile([P, J], U8, name="y_plane", align_bytes=64)
-        for h, copy in enumerate((nc.vector.tensor_copy, nc.scalar.copy)):
+        for slots, copy in ((slice(0, WOVEN_BY_VECTOR), nc.vector.tensor_copy), (slice(WOVEN_BY_VECTOR, J), nc.scalar.copy)):
             copy(
-                out=y_round[:, halves[h], :].rearrange("p (c i) t -> p c t i", i=4),
-                in_=y[:, :, halves[h]].rearrange("p t (c i) -> p c t i", i=4),
+                out=y_round[:, slots, :].rearrange("p (c i) t -> p c t i", i=4),
+                in_=y[:, :, slots].rearrange("p t (c i) -> p c t i", i=4),
             )
-        for h in range(2):
-            nc.vector.quantize_mx(
-                out=y_codes[:, halves[h]].bitcast(E4M3),
-                scales=y_plane[:, halves[h]],
-                in_=y_round[:, halves[h], :].rearrange("p j t -> p (j t)"),
-            )
+        nc.vector.quantize_mx(
+            out=y_codes[:].bitcast(E4M3), scales=y_plane[:], in_=y_round[:].rearrange("p j t -> p (j t)")
+        )
         nc.sync.dma_start(out=out_1[0].rearrange("p c t -> p (c t)").bitcast(I32), in_=y_codes[:].bitcast(I32))
-        for q in range(4):
+        for q in range(P // QUADRANT):
             queue = nc.scalar if q % 2 == 0 else nc.sync
             queue.dma_start(
-                out=out_2[0, 4 * q : 4 * q + 4, :].bitcast(I32), in_=y_plane[32 * q : 32 * q + 4, :].bitcast(I32)
+                out=out_2[0, 4 * q : 4 * q + 4, :].bitcast(I32),
+                in_=y_plane[QUADRANT * q : QUADRANT * q + 4, :].bitcast(I32),
             )

from contextlib import ExitStack

import concourse.mybir as mybir

K, T, J, R, N = 1024, 1024, 256, 512, 512
FLOPS = 2 * K * R * J + 2 * R * N * J

F32 = mybir.dt.float32
BF16 = mybir.dt.bfloat16
I32 = mybir.dt.int32
U32 = mybir.dt.uint32
U16 = mybir.dt.uint16
U8 = mybir.dt.uint8
E4M3 = mybir.dt.float8_e4m3fn_x4
E5M2 = mybir.dt.float8_e5m2_x4
E2M1 = mybir.dt.float4_e2m1fn_x4
ALU = mybir.AluOpType
ACT = mybir.ActivationFunctionType

P = 128
PACK = 4
PASSES = K // (P * PACK)
SHEETS = PASSES * PACK
QUADRANT = 32
ENTRIES = 16
LINE = 16
HALF = J // 2
QUARTER = J // 4
LAG = 2
EPS = 0.1

BOTH_ON_SCALAR = (1, 3, 4, 5)
BY_HALVES = (0, SHEETS - 3, SHEETS - 2, SHEETS - 1)
WOVEN_BY_VECTOR = 160


def deal(copy, dealt, raw, width):
    run = LINE // width
    copy(
        out=dealt.rearrange("p (t c i) -> p c t i", t=PACK, i=run),
        in_=raw.rearrange("p (c i t) -> p c t i", t=PACK, i=run),
    )


def load_scale_rows(queue, tile, rows, q):
    queue.dma_start(
        out=tile[QUADRANT * q : QUADRANT * q + 4, :, :].bitcast(I32),
        in_=rows[:, 4 * q : 4 * q + 4, :].rearrange("a s c -> s a c").bitcast(I32),
    )


def tile_list_pickgaps_lagged_levelled_pl_kernel(
    tc, xf, fk, w_words, w_scales, wb_words, wb_scales, rs, offs, offs2, out_0, out_1, out_2
):
    nc = tc.nc
    with ExitStack() as ctx:
        keep = ctx.enter_context(tc.tile_pool(name="keep", bufs=1))
        psum = ctx.enter_context(tc.psum_pool(name="psum", bufs=1))

        first = keep.tile([P, J // ENTRIES], U16, name="first")
        second = keep.tile([P, J // ENTRIES], U16, name="second")
        factor = keep.tile([P, PASSES, PACK], F32, name="factor")
        sheets = [keep.tile([P, T], F32, name=f"sheet{s}") for s in range(SHEETS)]
        w_raw = [keep.tile([P, 2 * R], U8, name=f"w_raw{a}") for a in range(PASSES)]
        w_scales_raw = keep.tile([P, PASSES, R], U8, name="w_scales_raw")
        wb_raw = keep.tile([P, N], U32, name="wb_raw", tag="wb_raw", align_bytes=64)
        wb_scales_raw = keep.tile([P, 1, N], U8, name="wb_scales_raw")
        resid = keep.tile([P, PACK, J], F32, name="resid")
        ha = keep.tile([P, (LAG + J) * PACK], F32, name="ha")

        nc.gpsimd.memset(w_scales_raw[:].bitcast(U32), 0)
        nc.gpsimd.memset(wb_scales_raw[:].bitcast(U32), 0)
        nc.gpsimd.memset(ha[:, 0 : LAG * PACK], 0.0)

        x_rows = xf.rearrange("(a p t) c -> a t p c", p=P, t=PACK)

        def load_sheet(s):
            nc.sync.dma_start(out=sheets[s][:], in_=x_rows[s // PACK, s % PACK])

        load_sheet(0)
        nc.sync.dma_start(second[:], offs2)
        nc.sync.dma_start(first[:], offs)
        for q in range(P // QUADRANT):
            load_scale_rows(nc.scalar, w_scales_raw, w_scales, q)
        load_sheet(1)
        load_sheet(2)
        nc.sync.dma_start(out=factor[:], in_=fk.rearrange("(a p t) o -> p a (t o)", p=P, t=PACK))
        for s in range(3, SHEETS):
            load_sheet(s)
        for a in range(PASSES):
            nc.sync.dma_start(out=w_raw[a][:].bitcast(I32), in_=w_words[a].bitcast(I32))
        nc.sync.dma_start(out=wb_raw[:].bitcast(I32), in_=wb_words[0].rearrange("p c t -> p (c t)").bitcast(I32))
        for q in range(P // QUADRANT):
            load_scale_rows(nc.sync, wb_scales_raw, wb_scales, q)
        nc.sync.dma_start(out=resid[:], in_=rs.rearrange("(p t) j -> p t j", t=PACK))

        one = keep.tile([P, 1], F32, name="one")
        unread = keep.tile([P, 1], F32, name="unread")
        nc.vector.memset(one[:], 1.0)
        nc.scalar.activation(out=unread[:], in_=one[:], func=ACT.Abs_reciprocal_sqrt)

        w_codes = [keep.tile([P, 2 * R], U8, name=f"w_codes{a}", align_bytes=64) for a in range(PASSES)]
        w_plane = keep.tile([P, PASSES, R], U8, name="w_plane", align_bytes=64)
        nc.vector.tensor_copy(
            out=w_plane[:].rearrange("p a (t c i) -> p a c t i", t=PACK, i=LINE),
            in_=w_scales_raw[:].rearrange("p a (c i t) -> p a c t i", t=PACK, i=LINE),
        )

        whole = slice(0, J)
        halves = [slice(h * HALF, (h + 1) * HALF) for h in range(2)]

        def picks(window, offsets, slots):
            return window[:].indirect(offsets[:, slots.start // ENTRIES : slots.stop // ENTRIES])

        u_codes = [keep.tile([P, J], U32, name=f"u_codes{a}", align_bytes=64) for a in range(PASSES)]
        u_plane = [keep.tile([P, J], U8, name=f"u_plane{a}", align_bytes=64) for a in range(PASSES)]
        for a in range(PASSES):
            u = keep.tile([P, J, PACK], BF16, name=f"u{a}", tag=f"u{a}", align_bytes=64)
            gaps = keep.tile([P, PACK, J], F32, name=f"gaps{a}")
            for t in range(PACK):
                s = a * PACK + t
                taken = keep.tile([P, J], F32, name=f"taken{s}")
                if s in BOTH_ON_SCALAR:
                    picked = keep.tile([P, J], F32, name=f"picked{s}")
                for slots in halves if s in BY_HALVES else [whole]:
                    nc.scalar.activation(out=taken[:, slots], in_=picks(sheets[s], second, slots), func=ACT.Copy)
                    if s in BOTH_ON_SCALAR:
                        nc.scalar.activation(out=picked[:, slots], in_=picks(sheets[s], first, slots), func=ACT.Copy)
                for slots in halves:
                    minuend = picked[:, slots] if s in BOTH_ON_SCALAR else picks(sheets[s], first, slots)
                    nc.vector.tensor_tensor(out=gaps[:, t, slots], in0=minuend, in1=taken[:, slots], op=ALU.subtract)
                for slots in halves:
                    nc.vector.tensor_scalar(
                        out=u[:, slots, t], in0=gaps[:, t, slots], scalar1=factor[:, a, t : t + 1],
                        scalar2=None, op0=ALU.mult,
                    )
            for slots in halves if a == PASSES - 1 else [whole]:
                nc.vector.quantize_mx(
                    out=u_codes[a][:, slots].bitcast(E4M3),
                    scales=u_plane[a][:, slots],
                    in_=u[:, slots, :].rearrange("p j t -> p (j t)"),
                )

        for a in range(PASSES):
            deal(nc.scalar.copy, w_codes[a][:].bitcast(U16), w_raw[a][:].bitcast(U16), 2)
        a_banks = [psum.tile([P, PACK, HALF], F32, name=f"a_bank{h}") for h in range(2)]
        for a in range(PASSES):
            for h, slots in enumerate(halves):
                for t in range(PACK):
                    nc.tensor.matmul_mx(
                        out=a_banks[h][:, t, :],
                        lhsT=w_codes[a][:, 2 * P * t : 2 * P * (t + 1)].bitcast(E2M1),
                        lhsT_scale=w_plane[:, a, P * t : P * (t + 1)],
                        rhs=u_codes[a][:, slots].bitcast(E4M3),
                        rhs_scale=u_plane[a][:, slots],
                        start=(a == 0 and t == 0),
                        stop=(a == PASSES - 1 and t == PACK - 1),
                    )

        wb_codes = keep.tile([P, N], U32, name="wb_codes", tag=f"u{PASSES - 1}", align_bytes=64)
        deal(nc.vector.tensor_copy, wb_codes[:].bitcast(I32), wb_raw[:].bitcast(I32), 4)
        wb_plane = keep.tile([P, N], U8, name="wb_plane", tag="wb_raw", align_bytes=64)
        deal(nc.vector.tensor_copy, wb_plane[:], wb_scales_raw[:, 0, :], 1)

        hid = keep.tile([P, J * PACK], BF16, name="hid", align_bytes=64)
        hid_codes = keep.tile([P, J], U32, name="hid_codes", align_bytes=64)
        hid_plane = keep.tile([P, J], U8, name="hid_plane", align_bytes=64)
        for j0 in range(0, J, QUARTER):
            now = ha[:, (LAG + j0) * PACK : (LAG + j0 + QUARTER) * PACK]
            before = ha[:, j0 * PACK : (j0 + QUARTER) * PACK]
            nc.scalar.activation(
                out=now.rearrange("p (j t) -> p j t", t=PACK),
                in_=a_banks[j0 // HALF][:, :, j0 % HALF : j0 % HALF + QUARTER].rearrange("p t j -> p j t"),
                func=ACT.Relu,
            )
            nc.vector.scalar_tensor_tensor(
                out=hid[:, j0 * PACK : (j0 + QUARTER) * PACK], in0=before, scalar=-0.5, in1=now,
                op0=ALU.mult, op1=ALU.add,
            )

        p_banks = [psum.tile([P, J], F32, name=f"p_bank{t}") for t in range(PACK)]
        for slots in halves:
            nc.vector.quantize_mx(
                out=hid_codes[:, slots].bitcast(E5M2),
                scales=hid_plane[:, slots],
                in_=hid[:, slots.start * PACK : slots.stop * PACK],
            )
            for t in range(PACK):
                nc.tensor.matmul_mx(
                    out=p_banks[t][:, slots],
                    lhsT=wb_codes[:, P * t : P * (t + 1)].bitcast(E5M2),
                    lhsT_scale=wb_plane[:, P * t : P * (t + 1)],
                    rhs=hid_codes[:, slots].bitcast(E5M2),
                    rhs_scale=hid_plane[:, slots],
                    start=True,
                    stop=True,
                )

        pb = keep.tile([P, PACK, J], F32, name="pb")
        squares = keep.tile([P, PACK, J], BF16, name="squares")
        total = keep.tile([P, PACK], F32, name="total")
        energy = keep.tile([P, PACK], F32, name="energy")
        mean = keep.tile([P, PACK], F32, name="mean")
        inverse = keep.tile([P, PACK], F32, name="inverse")
        y = keep.tile([P, PACK, J], F32, name="y")
        y_rows = out_0.rearrange("(p t) j -> p t j", t=PACK)
        groups = [slice(0, 2), slice(2, 3), slice(3, 4)]
        for group in groups:
            for t in range(group.start, group.stop):
                nc.vector.scalar_tensor_tensor(
                    out=pb[:, t, :], in0=p_banks[t][:], scalar=1.0, in1=resid[:, t, :],
                    op0=ALU.mult, op1=ALU.add, accum_out=total[:, t : t + 1],
                )
                nc.scalar.activation(
                    out=squares[:, t, :], in_=pb[:, t, :], func=ACT.Square,
                    scale=-float(J), bias=total[:, t : t + 1], accum_out=energy[:, t : t + 1],
                )
            nc.scalar.activation(
                out=inverse[:, group], in_=energy[:, group], func=ACT.Abs_reciprocal_sqrt, scale=1.0 / J**3, bias=EPS
            )
        nc.vector.tensor_scalar(out=mean[:], in0=total[:], scalar1=1.0 / J, scalar2=None, op0=ALU.mult)
        for t in range(PACK):
            nc.vector.tensor_scalar(
                out=y[:, t, :], in0=pb[:, t, :], scalar1=mean[:, t : t + 1], scalar2=inverse[:, t : t + 1],
                op0=ALU.subtract, op1=ALU.mult,
            )
            if t % 2 == 1:
                nc.sync.dma_start(out=y_rows[:, t - 1 : t + 1, :], in_=y[:, t - 1 : t + 1, :])

        y_round = keep.tile([P, J, PACK], BF16, name="y_round", align_bytes=64)
        y_codes = keep.tile([P, J], U32, name="y_codes", align_bytes=64)
        y_plane = keep.tile([P, J], U8, name="y_plane", align_bytes=64)
        for slots, copy in ((slice(0, WOVEN_BY_VECTOR), nc.vector.tensor_copy), (slice(WOVEN_BY_VECTOR, J), nc.scalar.copy)):
            copy(
                out=y_round[:, slots, :].rearrange("p (c i) t -> p c t i", i=4),
                in_=y[:, :, slots].rearrange("p t (c i) -> p c t i", i=4),
            )
        nc.vector.quantize_mx(
            out=y_codes[:].bitcast(E4M3), scales=y_plane[:], in_=y_round[:].rearrange("p j t -> p (j t)")
        )
        nc.sync.dma_start(out=out_1[0].rearrange("p c t -> p (c t)").bitcast(I32), in_=y_codes[:].bitcast(I32))
        for q in range(P // QUADRANT):
            queue = nc.scalar if q % 2 == 0 else nc.sync
            queue.dma_start(
                out=out_2[0, 4 * q : 4 * q + 4, :].bitcast(I32),
                in_=y_plane[QUADRANT * q : QUADRANT * q + 4, :].bitcast(I32),
            )
